import numpy as np
import ml_dtypes


def mxq(x, axis, fmt="e4m3"):
    dtype, down = {"e4m3": (ml_dtypes.float8_e4m3fn, 7), "e5m2": (ml_dtypes.float8_e5m2, 14)}[fmt]
    v = np.moveaxis(np.asarray(x, np.float32).astype(ml_dtypes.bfloat16).astype(np.float64), axis, -1)
    blocks = v.reshape(v.shape[:-1] + (-1, 32))
    amax = np.abs(blocks).max(-1, keepdims=True)
    byte = np.maximum(np.where(amax > 0, np.frexp(amax)[1] - 1 + 127, 0) - down, 1)
    scale = np.exp2(byte - 127.0)
    codes = (blocks / scale).astype(np.float32).astype(dtype).astype(np.float64)
    return np.moveaxis((codes * scale).reshape(v.shape), -1, axis)


WIDE = False


def mx_kscale(k):
    if not WIDE:
        return np.ones(k)
    levels = np.array([10, -10, 5, -5, 0])
    if k % 512:
        return np.exp2(np.random.permutation(np.resize(levels, k // 32))).repeat(32)
    a = np.empty((k // 512, 16))
    for p in range(k // 512):
        a[p, :8] = np.random.permutation(np.resize(levels, 8))
        for g in range(8):
            far = levels[np.abs(levels - a[p, g]) >= 10]
            a[p, g + 8] = far[np.random.randint(len(far))]
    return np.exp2(a.ravel()).repeat(32)


def f64(x):
    return np.asarray(x).astype(np.float64)


def striped(idx):
    return np.tile(idx.reshape(-1, 16).T, (8, 1)).astype(np.uint16)


def unstriped(offs):
    return offs[:16].T.reshape(-1).astype(np.int64)


def striped8(idx):
    return np.concatenate([x.reshape(-1, 16).T for x in idx]).astype(np.uint16)


def runs(offs, k):
    lists = np.stack([offs[16 * r : 16 * r + 16].T.reshape(-1) for r in range(8)]).astype(np.int64)
    return lists[np.arange(k) % 512 // 64]


def pack_weight(w):
    k, n = w.shape
    w = f64(np.asarray(w, np.float32).astype(ml_dtypes.bfloat16)).reshape(k // 32, 32, n)
    amax = np.abs(w).max(1)
    byte = np.clip(np.where(amax > 0, np.frexp(amax)[1] - 1 + 127 - 7, 1), 1, 254)
    scaled = (w * np.exp2(127.0 - byte)[:, None, :]).reshape(k, n).astype(np.float32)
    words = np.ascontiguousarray(scaled.reshape(k // 512, 128, 4, n).transpose(0, 1, 3, 2)).astype(ml_dtypes.float8_e4m3fn).view(np.uint8)
    return words, np.ascontiguousarray(byte.astype(np.uint8).reshape(k // 512, 16, n))


def unpack_weight(words, scales):
    g, p, n, _ = words.shape
    vals = np.ascontiguousarray(words).view(ml_dtypes.float8_e4m3fn).astype(np.float64) * np.repeat(np.exp2(scales.astype(np.float64) - 127.0), 8, axis=1)[..., None]
    return vals.transpose(0, 1, 3, 2).reshape(g * 512, n)


def sigmoid(v):
    return 1.0 / (1.0 + np.exp(-np.maximum(v, -700.0)))

def planes(y):
    n, m = y.shape
    v = y.astype(np.float32).astype(ml_dtypes.bfloat16).astype(np.float64).reshape(n // 32, 32, m)
    top = np.abs(v).max(1)
    byte = np.clip(np.where(top > 0, np.frexp(top)[1] - 1 + 127 - 7, 1), 1, 254)
    codes = (v * np.exp2(127.0 - byte)[:, None, :]).reshape(n, m).astype(np.float32).astype(ml_dtypes.float8_e4m3fn).view(np.uint8)
    words = codes.reshape(n // 512, 128, 4, m).transpose(0, 1, 3, 2)
    return np.ascontiguousarray(words), np.ascontiguousarray(byte.astype(np.uint8).reshape(n // 512, 16, m))


K, T, S, N, H, C = 512, 2048, 512, 512, 512, 512


def setup_inputs():
    n = np.random.standard_normal
    s = mx_kscale(K)[:, None]
    u = mx_kscale(S)
    packed_xT = pack_weight(n((K, T)) * s)
    packed_w1 = pack_weight(n((K, H)) / np.sqrt(K) / s)
    packed_w2 = pack_weight(n((H, N)) / np.sqrt(H) / u[:, None])
    return {
        "x_words": packed_xT[0],
        "x_scales": packed_xT[1],
        "w1_words": packed_w1[0],
        "w1_scales": packed_w1[1],
        "gn": (np.random.uniform(0.5, 1.5, (H, 1)) * u[:, None]).astype(np.float32),
        "w2_words": packed_w2[0],
        "w2_scales": packed_w2[1],
        "gs": (np.random.uniform(0.5, 1.5, (K, 1)) / s).astype(np.float32),
        "offs": striped(np.random.permutation(T)[:S]),
        "n1": striped8(np.stack([np.random.permutation(S) for _ in range(8)])),
        "n2": striped8(np.stack([np.random.permutation(S) for _ in range(8)])),
        "n3": striped8(np.stack([np.random.permutation(S) for _ in range(8)])),
        "n4": striped8(np.stack([np.random.permutation(S) for _ in range(8)])),
        "n5": striped8(np.stack([np.random.permutation(S) for _ in range(8)])),
        "cand": striped(np.random.permutation(T)[:C]),
        "n6": striped(np.random.permutation(S)),
        "n7": striped(np.random.permutation(S)),
    }


def reference(x_words, x_scales, w1_words, w1_scales, gn, w2_words, w2_scales, gs, offs, n1, n2, n3, n4, n5, cand, n6, n7):
    xq = unpack_weight(x_words, x_scales)[:, unstriped(offs)]
    y = unpack_weight(w1_words, w1_scales).T @ xq
    pa = y[np.arange(H)[:, None], runs(n1, H)]
    z = f64(gn) * (pa + (sigmoid(y[np.arange(H)[:, None], runs(n2, H)])) * (y[np.arange(H)[:, None], runs(n3, H)] - pa))
    a = unpack_weight(w2_words, w2_scales).T @ mxq(z, 0, "e4m3")
    x_cand = unpack_weight(x_words, x_scales)[:, unstriped(cand)]
    st = y[np.arange(H)[:, None], runs(n4, H)] - y
    z2 = f64(gs) * (y * (sigmoid(st[np.arange(H)[:, None], runs(n5, H)])))
    b = 0.0625 * ((x_cand.T @ mxq(z2, 0, "e4m3")))
    out_0 = (a + a[:, unstriped(n6)]) * (sigmoid(b + b[:, unstriped(n7)]))
    return (out_0,) + planes(out_0)

@@ -1,0 +1,256 @@
+from contextlib import ExitStack
+
+import concourse.mybir as mybir
+
+K, T, S = 512, 2048, 512
+FLOPS = 3 * 2 * 512 * 512 * 512
+
+F32 = mybir.dt.float32
+BF16 = mybir.dt.bfloat16
+I32 = mybir.dt.int32
+U32 = mybir.dt.uint32
+U16 = mybir.dt.uint16
+U8 = mybir.dt.uint8
+FP8X4 = mybir.dt.float8_e4m3fn_x4
+ACT = mybir.ActivationFunctionType
+ALU = mybir.AluOpType
+
+P = 128
+PACK = 4
+QUADS = 4
+SPLIT1 = 512
+SPLIT2 = 256
+NV = 2
+NVA = 4
+CANDT = 0
+YB = 1
+BDMA = 2
+W2T = 2
+HOLD = 1
+NB = 2
+AV = 2
+AE = 2
+SW1 = 1
+SW2 = 0
+LASTV = 1
+OUT_CHUNKS = ((0,256),(256,512))
+
+
+def tile_picked_fkcdtrieblerphopd_none_po_kernel(
+    tc, x_words, x_scales, w1_words, w1_scales, gn, w2_words, w2_scales, gs,
+    offs, n1, n2, n3, n4, n5, cand, n6, n7, out_0, out_1, out_2,
+):
+    nc = tc.nc
+    with ExitStack() as ctx:
+        keep = ctx.enter_context(tc.tile_pool(name="keep", bufs=1))
+        psum = ctx.enter_context(tc.psum_pool(name="psum", bufs=1))
+
+        def tile(shape, dtype, name):
+            return keep.tile(shape, dtype, name=name, align_bytes=64)
+
+        def tiles(shape, dtype, name):
+            return [tile(shape, dtype, "%s%d" % (name, t)) for t in range(PACK)]
+
+        def load_list(src, name):
+            dst = keep.tile([P, S // 16], U16, name=name)
+            nc.sync.dma_start(dst[:], src)
+            return dst
+
+        def load_words(src, name, queue):
+            dst = tile([P, src.shape[2]], U32, name)
+            queue.dma_start(dst[:].bitcast(I32), src[0].rearrange("p n r -> p (n r)").bitcast(I32))
+            return dst
+
+        def load_scales(src, name, clear, queues):
+            dst = tile([P, src.shape[2]], U8, name)
+            clear.memset(dst[:].bitcast(I32), 0)
+            for q in range(QUADS):
+                queues[q].dma_start(dst[32 * q : 32 * q + 4, :].bitcast(I32), src[0, 4 * q : 4 * q + 4, :].bitcast(I32))
+            return dst
+
+        def load_gain(src, name):
+            dst = tile([P, PACK], F32, name)
+            nc.sync.dma_start(dst[:], src.rearrange("(p t) one -> p (t one)", t=PACK))
+            return dst
+
+        def deal(src, name, copy):
+            dst = tile([P, S], src.dtype, name)
+            copy(
+                out=dst[:].rearrange("p (t m) -> p t m", t=PACK),
+                in_=src[:].rearrange("p (m t) -> p t m", t=PACK),
+            )
+            return dst
+
+        def product(bank, words, scales, t, rhs_words, rhs_scales):
+            cols = slice(P * t, P * (t + 1))
+            nc.tensor.matmul_mx(
+                out=bank[:], lhsT=words[:, cols].bitcast(FP8X4), lhsT_scale=scales[:, cols],
+                rhs=rhs_words[:].bitcast(FP8X4), rhs_scale=rhs_scales[:], start=True, stop=True,
+            )
+
+        def interleave(copy, dst, src):
+            copy(
+                out=dst.rearrange("p (c i) t -> p c t i", i=4),
+                in_=src.rearrange("p t (c i) -> p c t i", i=4),
+            )
+
+        def split_interleave(dst, src, cut):
+            if cut > 0:
+                interleave(nc.scalar.copy, dst[:, :cut, :], src[:, :, :cut])
+            if cut < S:
+                interleave(nc.vector.tensor_copy, dst[:, cut:, :], src[:, :, cut:])
+
+        def quantise(words, scales, grouped):
+            nc.vector.quantize_mx(out=words.bitcast(FP8X4), scales=scales, in_=grouped.rearrange("p j t -> p (j t)"))
+
+        l_offs = load_list(offs, "l_offs")
+        xw = load_words(x_words, "xw", nc.scalar)
+        w1s_raw = load_scales(w1_scales, "w1s_raw", nc.gpsimd, [nc.sync, nc.sync, nc.gpsimd, nc.gpsimd])
+        xs = load_scales(x_scales, "xs", nc.vector, [nc.sync] * QUADS)
+        w1w_raw = load_words(w1_words, "w1w_raw", nc.sync)
+        l2 = load_list(n2, "l2")
+        l1 = load_list(n1, "l1")
+        l3 = load_list(n3, "l3")
+        l_cand = load_list(cand, "l_cand")
+        gn_t = load_gain(gn, "gn_t")
+        l4 = load_list(n4, "l4")
+        l5 = load_list(n5, "l5")
+        gs_t = load_gain(gs, "gs_t")
+        w2w_raw = load_words(w2_words, "w2w_raw", nc.sync)
+        l6 = load_list(n6, "l6")
+        l7 = load_list(n7, "l7")
+
+        y_win = tiles([P, 2 * S], F32, "y_win")
+        for t in range(PACK):
+            nc.gpsimd.memset(y_win[t][:, S:], 0.0)
+        w2s_raw = load_scales(w2_scales, "w2s_raw", nc.gpsimd, [nc.gpsimd] * QUADS)
+
+        xq_s = tile([P, S], U8, "xq_s")
+        nc.vector.tensor_copy(out=xq_s[:], in_=xs[:].indirect(l_offs[:]))
+        w1w = deal(w1w_raw, "w1w", nc.scalar.copy if SW1 else nc.vector.tensor_copy)
+        w1s = deal(w1s_raw, "w1s", nc.vector.tensor_copy)
+        xq_w = tile([P, S], U32, "xq_w")
+        nc.vector.tensor_copy(out=xq_w[:], in_=xw[:].indirect(l_offs[:]))
+
+        st_win = tiles([P, 2 * S], F32, "st_win")
+        a_win = tiles([P, 2 * S], F32, "a_win")
+        b_win = tiles([P, 2 * S], F32, "b_win")
+        s2 = [x[:] for x in tiles([P, S], F32, "s2")]
+        d = [x[:] for x in tiles([P, S], F32, "d")]
+        e = [x[:] for x in tiles([P, S], F32, "e")]
+        pa = [a_win[t][:, S:] for t in range(PACK)]
+        if HOLD:
+            e[2] = st_win[0][:, :S]
+            pa[3] = st_win[1][:, :S]
+            e[3] = st_win[2][:, :S]
+            s2[3] = st_win[3][:, S:]
+            d[3] = a_win[3][:, S:]
+        z = tile([P, PACK, S], F32, "z")
+        xc_s = tile([P, S], U8, "xc_s")
+        xc_w = tile([P, S], U32, "xc_w")
+        for t in range(PACK):
+            gain = gn_t[:, t : t + 1]
+            y_bank = psum.tile([P, S], F32, name="yb%d" % t, tag="yb%d" % (t % YB))
+            product(y_bank, w1w, w1s, t, xq_w, xq_s)
+            if t == 0:
+                nc.vector.tensor_copy(out=y_win[t][:, :S], in_=y_bank[:])
+                nc.scalar.activation(out=s2[t], in_=y_win[t][:].indirect(l2[:]), func=ACT.Sigmoid)
+            else:
+                nc.scalar.copy(out=y_win[t][:, :S], in_=y_bank[:])
+            nc.scalar.activation(out=pa[t], in_=y_win[t][:].indirect(l1[:]), func=ACT.Copy)
+            if t > 0:
+                nc.scalar.activation(out=s2[t], in_=y_win[t][:].indirect(l2[:]), func=ACT.Sigmoid)
+            nc.vector.tensor_tensor(out=d[t], in0=y_win[t][:].indirect(l3[:]), in1=pa[t], op=ALU.subtract)
+            nc.vector.scalar_tensor_tensor(out=e[t], in0=d[t], scalar=gain, in1=s2[t], op0=ALU.mult, op1=ALU.mult)
+            nc.vector.scalar_tensor_tensor(out=z[:, t, :], in0=pa[t], scalar=gain, in1=e[t], op0=ALU.mult, op1=ALU.add)
+            nc.sync.dma_start(st_win[t][:, S:], y_win[t][:, :S])
+            if t == CANDT:
+                nc.vector.tensor_copy(out=xc_s[:].rearrange("p (t m) -> p m t", t=PACK), in_=xs[:].indirect(l_cand[:]))
+                nc.vector.tensor_copy(out=xc_w[:].rearrange("p (t m) -> p m t", t=PACK), in_=xw[:].indirect(l_cand[:]))
+            if t == W2T:
+                w2w = deal(w2w_raw, "w2w", nc.scalar.copy if SW2 else nc.vector.tensor_copy)
+                w2s = deal(w2s_raw, "w2s", nc.vector.tensor_copy)
+
+        z_bf = tile([P, S, PACK], BF16, "z_bf")
+        zq_w = tile([P, S], U32, "zq_w")
+        zq_s = tile([P, S], U8, "zq_s")
+        split_interleave(z_bf, z, SPLIT1)
+        quantise(zq_w[:], zq_s[:], z_bf[:])
+        a_bank = [psum.tile([P, S], F32, name="ab%d" % t, tag="ab%d" % t) for t in range(PACK)]
+        for t in range(PACK):
+            product(a_bank[t], w2w, w2s, t, zq_w, zq_s)
+
+        def fetch_a(t):
+            nc.scalar.copy(out=a_win[t][:, :S], in_=a_bank[t][:])
+            if t < AV:
+                nc.vector.tensor_copy(out=b_win[t][:, S:], in_=a_win[t][:, :S])
+            else:
+                nc.sync.dma_start(b_win[t][:, S:], a_win[t][:, :S])
+
+        s5 = tiles([P, S], F32, "s5")
+        z2 = tile([P, PACK, S], F32, "z2")
+        for t in range(PACK):
+            y_plain = st_win[t][:, S:]
+            nc.vector.tensor_tensor(out=st_win[t][:, :S], in0=y_win[t][:].indirect(l4[:]), in1=y_plain, op=ALU.subtract)
+            if t == PACK - 1:
+                for u in range(AE):
+                    fetch_a(u)
+            nc.scalar.activation(out=s5[t][:], in_=st_win[t][:].indirect(l5[:]), func=ACT.Sigmoid)
+            nc.vector.scalar_tensor_tensor(
+                out=z2[:, t, :], in0=y_plain, scalar=gs_t[:, t : t + 1], in1=s5[t][:], op0=ALU.mult, op1=ALU.mult)
+
+        z2_bf = tile([P, S, PACK], BF16, "z2_bf")
+        z2q_w = tile([P, S], U32, "z2q_w")
+        z2q_s = tile([P, S], U8, "z2q_s")
+        split_interleave(z2_bf, z2, SPLIT2)
+        quantise(z2q_w[:], z2q_s[:], z2_bf[:])
+        for u in range(AE, PACK):
+            fetch_a(u)
+        b_plain = tiles([P, S], F32, "b_plain")
+        for t in range(PACK):
+            b_bank = psum.tile([P, S], F32, name="bb%d" % t, tag="bb%d" % (t % 3))
+            product(b_bank, xc_w, xc_s, t, z2q_w, z2q_s)
+            nc.scalar.copy(out=b_win[t][:, :S], in_=b_bank[:])
+            if t < NV:
+                if t >= NV - BDMA:
+                    nc.sync.dma_start(b_plain[t][:], b_win[t][:, :S])
+                else:
+                    nc.vector.tensor_copy(out=b_plain[t][:], in_=b_win[t][:, :S])
+
+        sa = tile([P, PACK, S], F32, "sa")
+        for t in range(PACK):
+            if t < NVA:
+                nc.vector.tensor_tensor(out=sa[:, t, :], in0=a_win[t][:].indirect(l6[:]), in1=b_win[t][:, S:], op=ALU.add)
+            else:
+                nc.scalar.activation(out=d[t], in_=a_win[t][:].indirect(l6[:]), func=ACT.Copy)
+                nc.vector.tensor_tensor(out=sa[:, t, :], in0=d[t], in1=a_win[t][:, :S], op=ALU.add)
+
+        out_rows = out_0.rearrange("(p t) j -> p t j", t=PACK)
+        out_words = out_1[0].rearrange("p n r -> p (n r)").bitcast(I32)
+        oq_s = tile([P, S], U8, "oq_s")
+        sb_buf = tiles([P, PACK, 256], F32, "sb")
+        gb_buf = tiles([P, PACK, 256], F32, "gb")
+        for c0, c1 in OUT_CHUNKS:
+            w = c1 - c0
+            sb = sb_buf[OUT_CHUNKS.index((c0, c1)) % NB][:, :, :w]
+            gb = gb_buf[OUT_CHUNKS.index((c0, c1)) % NB][:, :, :w]
+            for t in range(PACK):
+                picked = b_win[t][:].indirect(l7[:, c0 // 16 : c1 // 16])
+                if t < NV:
+                    nc.vector.tensor_tensor(out=sb[:, t, :], in0=picked, in1=b_plain[t][:, c0:c1], op=ALU.add)
+                else:
+                    nc.scalar.activation(out=gb[:, t, :], in_=picked, func=ACT.Copy)
+                    nc.vector.tensor_tensor(out=sb[:, t, :], in0=gb[:, t, :], in1=b_win[t][:, c0:c1], op=ALU.add)
+            gate = tile([P, PACK, w], F32, "gate%d" % c0)
+            nc.scalar.activation(out=gate[:], in_=sb, func=ACT.Sigmoid, scale=0.0625)
+            res = tile([P, PACK, w], F32, "res%d" % c0)
+            nc.vector.tensor_tensor(out=res[:], in0=sa[:, :, c0:c1], in1=gate[:], op=ALU.mult)
+            nc.sync.dma_start(out_rows[:, :, c0:c1], res[:])
+            res_bf = tile([P, w, PACK], BF16, "res_bf%d" % c0)
+            interleave(nc.vector.tensor_copy if c1 == S and LASTV else nc.scalar.copy, res_bf[:], res[:])
+            oq_w = tile([P, w], U32, "oq_w%d" % c0)
+            quantise(oq_w[:], oq_s[:, c0:c1], res_bf[:])
+            nc.sync.dma_start(out_words[:, c0:c1], oq_w[:].bitcast(I32))
+        for q in range(QUADS):
+            queue = nc.scalar if q % 2 else nc.sync
+            queue.dma_start(out_2[0, 4 * q : 4 * q + 4, :].bitcast(I32), oq_s[32 * q : 32 * q + 4, :].bitcast(I32))

@@ -25,12 +25,38 @@ NVA = 4
 CANDT = 0
 YB = 1
 BDMA = 2
-W2T = 2
-HOLD = 1
+W2T = 5
+DINB = 1
+XH = 0
+GH = 0
+AH = 0
+CE = 0
+PAV = 0
+YBK = (0,0,0,0)
+LY = -2
+LPA = 1
+LS2 = 1
+LD = 1
+LST = 0
+LS5 = 3
+LE = 2
+LZ = 2
+LZ2 = 6
+ZQ = 6
+HA = "vvdd"
+HB = "vsss"
+BFIRST = 1
+ACH = 1
+BCH = 1
+QW1S = "ssss"
+QW1W = "a"
+QG = "g"
+QW2W = "s"
+QW2S = "ssss"
 NB = 2
 AV = 2
-AE = 2
-SW1 = 1
+AE = 1
+SW1 = 0
 SW2 = 0
 LASTV = 1
 OUT_CHUNKS = ((0,256),(256,512))
@@ -61,16 +87,18 @@ def tile_picked_fkcdtrieblerphopd_none_po_kernel(
             queue.dma_start(dst[:].bitcast(I32), src[0].rearrange("p n r -> p (n r)").bitcast(I32))
             return dst
 
-        def load_scales(src, name, clear, queues):
+        def load_scales(src, name, clears, queues):
             dst = tile([P, src.shape[2]], U8, name)
-            clear.memset(dst[:].bitcast(I32), 0)
+            share = src.shape[2] // len(clears)
+            for i, clear in enumerate(clears):
+                clear.memset(dst[:, i * share : (i + 1) * share].bitcast(I32), 0)
             for q in range(QUADS):
                 queues[q].dma_start(dst[32 * q : 32 * q + 4, :].bitcast(I32), src[0, 4 * q : 4 * q + 4, :].bitcast(I32))
             return dst
 
-        def load_gain(src, name):
+        def load_gain(src, name, queue):
             dst = tile([P, PACK], F32, name)
-            nc.sync.dma_start(dst[:], src.rearrange("(p t) one -> p (t one)", t=PACK))
+            queue.dma_start(dst[:], src.rearrange("(p t) one -> p (t one)", t=PACK))
             return dst
 
         def deal(src, name, copy):
@@ -103,27 +131,27 @@ def tile_picked_fkcdtrieblerphopd_none_po_kernel(
         def quantise(words, scales, grouped):
             nc.vector.quantize_mx(out=words.bitcast(FP8X4), scales=scales, in_=grouped.rearrange("p j t -> p (j t)"))
 
+        Q = {"s": nc.sync, "a": nc.scalar, "g": nc.gpsimd}
         l_offs = load_list(offs, "l_offs")
-        xw = load_words(x_words, "xw", nc.scalar)
-        w1s_raw = load_scales(w1_scales, "w1s_raw", nc.gpsimd, [nc.sync, nc.sync, nc.gpsimd, nc.gpsimd])
-        xs = load_scales(x_scales, "xs", nc.vector, [nc.sync] * QUADS)
-        w1w_raw = load_words(w1_words, "w1w_raw", nc.sync)
+        w1w_raw = load_words(w1_words, "w1w_raw", nc.scalar)
+        xs = load_scales(x_scales, "xs", [nc.vector, nc.gpsimd], [nc.sync] * QUADS)
+        xw = load_words(x_words, "xw", nc.sync)
+        if CE:
+            l_cand = load_list(cand, "l_cand")
+        gn_t = load_gain(gn, "gn_t", Q[QG])
+        gs_t = load_gain(gs, "gs_t", Q[QG])
+        w1s_raw = load_scales(w1_scales, "w1s_raw", [nc.gpsimd], [Q[c] for c in QW1S])
         l2 = load_list(n2, "l2")
         l1 = load_list(n1, "l1")
         l3 = load_list(n3, "l3")
-        l_cand = load_list(cand, "l_cand")
-        gn_t = load_gain(gn, "gn_t")
+        if not CE:
+            l_cand = load_list(cand, "l_cand")
         l4 = load_list(n4, "l4")
         l5 = load_list(n5, "l5")
-        gs_t = load_gain(gs, "gs_t")
-        w2w_raw = load_words(w2_words, "w2w_raw", nc.sync)
-        l6 = load_list(n6, "l6")
-        l7 = load_list(n7, "l7")
 
         y_win = tiles([P, 2 * S], F32, "y_win")
         for t in range(PACK):
-            nc.gpsimd.memset(y_win[t][:, S:], 0.0)
-        w2s_raw = load_scales(w2_scales, "w2s_raw", nc.gpsimd, [nc.gpsimd] * QUADS)
+            (nc.vector if t == 0 else nc.gpsimd).memset(y_win[t][:, S:], 0.0)
 
         xq_s = tile([P, S], U8, "xq_s")
         nc.vector.tensor_copy(out=xq_s[:], in_=xs[:].indirect(l_offs[:]))
@@ -135,116 +163,161 @@ def tile_picked_fkcdtrieblerphopd_none_po_kernel(
         st_win = tiles([P, 2 * S], F32, "st_win")
         a_win = tiles([P, 2 * S], F32, "a_win")
         b_win = tiles([P, 2 * S], F32, "b_win")
-        s2 = [x[:] for x in tiles([P, S], F32, "s2")]
-        d = [x[:] for x in tiles([P, S], F32, "d")]
-        e = [x[:] for x in tiles([P, S], F32, "e")]
+        s2 = tiles([P, S], F32, "s2")
+        s5 = tiles([P, S], F32, "s5")
+        e = tiles([P, S], F32, "e")
         pa = [a_win[t][:, S:] for t in range(PACK)]
-        if HOLD:
-            e[2] = st_win[0][:, :S]
-            pa[3] = st_win[1][:, :S]
-            e[3] = st_win[2][:, :S]
-            s2[3] = st_win[3][:, S:]
-            d[3] = a_win[3][:, S:]
+        if not DINB:
+            dd = [x[:] for x in tiles([P, S], F32, "d")]
+        else:
+            dd = [b_win[t][:, S:] for t in range(PACK)]
         z = tile([P, PACK, S], F32, "z")
+        z2 = tile([P, PACK, S], F32, "z2")
         xc_s = tile([P, S], U8, "xc_s")
-        xc_w = tile([P, S], U32, "xc_w")
-        for t in range(PACK):
-            gain = gn_t[:, t : t + 1]
-            y_bank = psum.tile([P, S], F32, name="yb%d" % t, tag="yb%d" % (t % YB))
+        xc_w = keep.tile([P, S], U32, name="xc_w", tag="w1s_raw" if XH else "xc_w", align_bytes=64)
+
+        def f_y(t):
+            y_bank = psum.tile([P, S], F32, name="yb%d" % t, tag="yb%d" % YBK[t])
             product(y_bank, w1w, w1s, t, xq_w, xq_s)
             if t == 0:
                 nc.vector.tensor_copy(out=y_win[t][:, :S], in_=y_bank[:])
-                nc.scalar.activation(out=s2[t], in_=y_win[t][:].indirect(l2[:]), func=ACT.Sigmoid)
             else:
                 nc.scalar.copy(out=y_win[t][:, :S], in_=y_bank[:])
-            nc.scalar.activation(out=pa[t], in_=y_win[t][:].indirect(l1[:]), func=ACT.Copy)
-            if t > 0:
-                nc.scalar.activation(out=s2[t], in_=y_win[t][:].indirect(l2[:]), func=ACT.Sigmoid)
-            nc.vector.tensor_tensor(out=d[t], in0=y_win[t][:].indirect(l3[:]), in1=pa[t], op=ALU.subtract)
-            nc.vector.scalar_tensor_tensor(out=e[t], in0=d[t], scalar=gain, in1=s2[t], op0=ALU.mult, op1=ALU.mult)
-            nc.vector.scalar_tensor_tensor(out=z[:, t, :], in0=pa[t], scalar=gain, in1=e[t], op0=ALU.mult, op1=ALU.add)
             nc.sync.dma_start(st_win[t][:, S:], y_win[t][:, :S])
-            if t == CANDT:
+
+        def f_pa(t):
+            if t < PAV:
+                nc.vector.tensor_copy(out=pa[t], in_=y_win[t][:].indirect(l1[:]))
+            else:
+                nc.scalar.activation(out=pa[t], in_=y_win[t][:].indirect(l1[:]), func=ACT.Copy)
+
+        def f_s2(t):
+            nc.scalar.activation(out=s2[t][:], in_=y_win[t][:].indirect(l2[:]), func=ACT.Sigmoid)
+
+        def f_d(t):
+            nc.vector.tensor_tensor(out=dd[t], in0=y_win[t][:].indirect(l3[:]), in1=pa[t], op=ALU.subtract)
+
+        def f_e(t):
+            nc.vector.scalar_tensor_tensor(out=e[t][:], in0=dd[t], scalar=gn_t[:, t : t + 1], in1=s2[t][:], op0=ALU.mult, op1=ALU.mult)
+
+        def f_z(t):
+            nc.vector.scalar_tensor_tensor(out=z[:, t, :], in0=pa[t], scalar=gn_t[:, t : t + 1], in1=e[t][:], op0=ALU.mult, op1=ALU.add)
+
+        def f_st(t):
+            nc.vector.tensor_tensor(out=st_win[t][:, :S], in0=y_win[t][:].indirect(l4[:]), in1=st_win[t][:, S:], op=ALU.subtract)
+
+        def f_s5(t):
+            nc.scalar.activation(out=s5[t][:], in_=st_win[t][:].indirect(l5[:]), func=ACT.Sigmoid)
+
+        def f_z2(t):
+            nc.vector.scalar_tensor_tensor(
+                out=z2[:, t, :], in0=y_win[t][:, :S], scalar=gs_t[:, t : t + 1], in1=s5[t][:], op0=ALU.mult, op1=ALU.mult)
+
+        f_y(0)
+        f_s2(0)
+        stages = [(f_y, LY), (f_pa, LPA), (f_s2, LS2), (f_d, LD), (f_st, LST), (f_s5, LS5), (f_e, LE), (f_z, LZ), (f_z2, LZ2)]
+        for step in range(-4, 20):
+            for f, lag in stages:
+                t = step - lag
+                if 0 <= t < PACK and not (t == 0 and f in (f_y, f_s2)):
+                    f(t)
+            if step == CANDT:
                 nc.vector.tensor_copy(out=xc_s[:].rearrange("p (t m) -> p m t", t=PACK), in_=xs[:].indirect(l_cand[:]))
                 nc.vector.tensor_copy(out=xc_w[:].rearrange("p (t m) -> p m t", t=PACK), in_=xw[:].indirect(l_cand[:]))
-            if t == W2T:
+            if step == W2T:
+                w2w_raw = load_words(w2_words, "w2w_raw", Q[QW2W])
+                w2s_raw = load_scales(w2_scales, "w2s_raw", [nc.gpsimd], [Q[c] for c in QW2S])
                 w2w = deal(w2w_raw, "w2w", nc.scalar.copy if SW2 else nc.vector.tensor_copy)
                 w2s = deal(w2s_raw, "w2s", nc.vector.tensor_copy)
+            if step == ZQ:
+                z_bf = tile([P, S, PACK], BF16, "z_bf")
+                zq_w = tile([P, S], U32, "zq_w")
+                zq_s = tile([P, S], U8, "zq_s")
+                split_interleave(z_bf, z, SPLIT1)
+                quantise(zq_w[:], zq_s[:], z_bf[:])
 
-        z_bf = tile([P, S, PACK], BF16, "z_bf")
-        zq_w = tile([P, S], U32, "zq_w")
-        zq_s = tile([P, S], U8, "zq_s")
-        split_interleave(z_bf, z, SPLIT1)
-        quantise(zq_w[:], zq_s[:], z_bf[:])
-        a_bank = [psum.tile([P, S], F32, name="ab%d" % t, tag="ab%d" % t) for t in range(PACK)]
-        for t in range(PACK):
-            product(a_bank[t], w2w, w2s, t, zq_w, zq_s)
+        l6 = load_list(n6, "l6")
+        l7 = load_list(n7, "l7")
 
-        def fetch_a(t):
-            nc.scalar.copy(out=a_win[t][:, :S], in_=a_bank[t][:])
-            if t < AV:
-                nc.vector.tensor_copy(out=b_win[t][:, S:], in_=a_win[t][:, :S])
-            else:
-                nc.sync.dma_start(b_win[t][:, S:], a_win[t][:, :S])
+        def fetch(t, bank, win, plain, how):
+            (nc.vector.tensor_copy if how in "W" else nc.scalar.copy)(out=win[:, :S], in_=bank[:])
+            if how == "v":
+                nc.vector.tensor_copy(out=plain, in_=win[:, :S])
+            if how in "dW":
+                nc.sync.dma_start(plain, win[:, :S])
 
-        s5 = tiles([P, S], F32, "s5")
-        z2 = tile([P, PACK, S], F32, "z2")
-        for t in range(PACK):
-            y_plain = st_win[t][:, S:]
-            nc.vector.tensor_tensor(out=st_win[t][:, :S], in0=y_win[t][:].indirect(l4[:]), in1=y_plain, op=ALU.subtract)
-            if t == PACK - 1:
-                for u in range(AE):
-                    fetch_a(u)
-            nc.scalar.activation(out=s5[t][:], in_=st_win[t][:].indirect(l5[:]), func=ACT.Sigmoid)
-            nc.vector.scalar_tensor_tensor(
-                out=z2[:, t, :], in0=y_plain, scalar=gs_t[:, t : t + 1], in1=s5[t][:], op0=ALU.mult, op1=ALU.mult)
+        a_plain = tiles([P, S], F32, "a_plain")
+        b_plain = tiles([P, S], F32, "b_plain")
 
+        def f_a(t):
+            a_bank = psum.tile([P, S], F32, name="ab%d" % t, tag="ab%d" % t)
+            product(a_bank, w2w, w2s, t, zq_w, zq_s)
+            fetch(t, a_bank, a_win[t], a_plain[t][:], HA[t])
+
+        for t in range(AE):
+            f_a(t)
         z2_bf = tile([P, S, PACK], BF16, "z2_bf")
         z2q_w = tile([P, S], U32, "z2q_w")
         z2q_s = tile([P, S], U8, "z2q_s")
         split_interleave(z2_bf, z2, SPLIT2)
         quantise(z2q_w[:], z2q_s[:], z2_bf[:])
-        for u in range(AE, PACK):
-            fetch_a(u)
-        b_plain = tiles([P, S], F32, "b_plain")
-        for t in range(PACK):
-            b_bank = psum.tile([P, S], F32, name="bb%d" % t, tag="bb%d" % (t % 3))
-            product(b_bank, xc_w, xc_s, t, z2q_w, z2q_s)
-            nc.scalar.copy(out=b_win[t][:, :S], in_=b_bank[:])
-            if t < NV:
-                if t >= NV - BDMA:
-                    nc.sync.dma_start(b_plain[t][:], b_win[t][:, :S])
-                else:
-                    nc.vector.tensor_copy(out=b_plain[t][:], in_=b_win[t][:, :S])
 
-        sa = tile([P, PACK, S], F32, "sa")
-        for t in range(PACK):
-            if t < NVA:
-                nc.vector.tensor_tensor(out=sa[:, t, :], in0=a_win[t][:].indirect(l6[:]), in1=b_win[t][:, S:], op=ALU.add)
+        def f_b(t):
+            b_bank = psum.tile([P, S], F32, name="bb%d" % t, tag="bb%d" % (t % 2))
+            product(b_bank, xc_w, xc_s, t, z2q_w, z2q_s)
+            fetch(t, b_bank, b_win[t], b_plain[t][:], HB[t])
+
+        if BFIRST:
+            for t in range(PACK):
+                f_b(t)
+        for t in range(AE, PACK):
+            f_a(t)
+        if not BFIRST:
+            for t in range(PACK):
+                f_b(t)
+
+        def add_picked(out, spare, win, plain, lst, c0, c1, how):
+            picked = win[:].indirect(lst[:, c0 // 16 : c1 // 16])
+            if how == "s":
+                nc.scalar.activation(out=spare, in_=picked, func=ACT.Copy)
+                nc.vector.tensor_tensor(out=out, in0=spare, in1=win[:, c0:c1], op=ALU.add)
             else:
-                nc.scalar.activation(out=d[t], in_=a_win[t][:].indirect(l6[:]), func=ACT.Copy)
-                nc.vector.tensor_tensor(out=sa[:, t, :], in0=d[t], in1=a_win[t][:, :S], op=ALU.add)
+                nc.vector.tensor_tensor(out=out, in0=picked, in1=plain[:, c0:c1], op=ALU.add)
+
+        if not ACH:
+            sa = tile([P, PACK, S], F32, "sa")
+            ga = tile([P, PACK, S], F32, "ga")
+            for t in range(PACK):
+                add_picked(sa[:, t, :], ga[:, t, :], a_win[t], a_plain[t], l6, 0, S, HA[t])
+        if not BCH:
+            sb = tile([P, PACK, S], F32, "sb")
+            gb = tile([P, PACK, S], F32, "gb")
+            for t in range(PACK):
+                add_picked(sb[:, t, :], gb[:, t, :], b_win[t], b_plain[t], l7, 0, S, HB[t])
 
         out_rows = out_0.rearrange("(p t) j -> p t j", t=PACK)
         out_words = out_1[0].rearrange("p n r -> p (n r)").bitcast(I32)
         oq_s = tile([P, S], U8, "oq_s")
-        sb_buf = tiles([P, PACK, 256], F32, "sb")
-        gb_buf = tiles([P, PACK, 256], F32, "gb")
         for c0, c1 in OUT_CHUNKS:
             w = c1 - c0
-            sb = sb_buf[OUT_CHUNKS.index((c0, c1)) % NB][:, :, :w]
-            gb = gb_buf[OUT_CHUNKS.index((c0, c1)) % NB][:, :, :w]
-            for t in range(PACK):
-                picked = b_win[t][:].indirect(l7[:, c0 // 16 : c1 // 16])
-                if t < NV:
-                    nc.vector.tensor_tensor(out=sb[:, t, :], in0=picked, in1=b_plain[t][:, c0:c1], op=ALU.add)
-                else:
-                    nc.scalar.activation(out=gb[:, t, :], in_=picked, func=ACT.Copy)
-                    nc.vector.tensor_tensor(out=sb[:, t, :], in0=gb[:, t, :], in1=b_win[t][:, c0:c1], op=ALU.add)
+            if not BCH:
+                sbc = sb[:, :, c0:c1]
+            if not ACH:
+                sac = sa[:, :, c0:c1]
+            if BCH:
+                sbc = tile([P, PACK, w], F32, "sb%d" % c0)[:]
+                gbc = keep.tile([P, PACK, w], F32, name="gb%d" % c0, tag=("sb0" if GH == 1 and c0 else "gb%d" % c0), align_bytes=64)
+                for t in range(PACK):
+                    add_picked(sbc[:, t, :], gbc[:, t, :], b_win[t], b_plain[t], l7, c0, c1, HB[t])
             gate = tile([P, PACK, w], F32, "gate%d" % c0)
-            nc.scalar.activation(out=gate[:], in_=sb, func=ACT.Sigmoid, scale=0.0625)
+            nc.scalar.activation(out=gate[:], in_=sbc, func=ACT.Sigmoid, scale=0.0625)
+            if ACH:
+                sac = keep.tile([P, PACK, w], F32, name="sa%d" % c0, tag=("sa0" if AH == 1 and c0 else "sb0" if AH == 2 and c0 else "sa%d" % c0), align_bytes=64)[:]
+                gac = tile([P, PACK, w], F32, "ga%d" % c0)
+                for t in range(PACK):
+                    add_picked(sac[:, t, :], gac[:, t, :], a_win[t], a_plain[t], l6, c0, c1, HA[t])
             res = tile([P, PACK, w], F32, "res%d" % c0)
-            nc.vector.tensor_tensor(out=res[:], in0=sa[:, :, c0:c1], in1=gate[:], op=ALU.mult)
+            nc.vector.tensor_tensor(out=res[:], in0=sac, in1=gate[:], op=ALU.mult)
             nc.sync.dma_start(out_rows[:, :, c0:c1], res[:])
             res_bf = tile([P, w, PACK], BF16, "res_bf%d" % c0)
             interleave(nc.vector.tensor_copy if c1 == S and LASTV else nc.scalar.copy, res_bf[:], res[:])

@@ -2,7 +2,6 @@ from contextlib import ExitStack
 
 import concourse.mybir as mybir
 
-K, T, S = 512, 2048, 512
 FLOPS = 3 * 2 * 512 * 512 * 512
 
 F32 = mybir.dt.float32
@@ -18,48 +17,13 @@ ALU = mybir.AluOpType
 P = 128
 PACK = 4
 QUADS = 4
-SPLIT1 = 512
-SPLIT2 = 256
-NV = 2
-NVA = 4
-CANDT = 0
-YB = 1
-BDMA = 2
-W2T = 5
-DINB = 1
-XH = 0
-GH = 0
-AH = 0
-CE = 0
-PAV = 0
-YBK = (0,0,0,0)
-LY = -2
-LPA = 1
-LS2 = 1
-LD = 1
-LST = 0
-LS5 = 3
-LE = 2
-LZ = 2
-LZ2 = 6
-ZQ = 6
-HA = "vvdd"
-HB = "vsss"
-BFIRST = 1
-ACH = 1
-BCH = 1
-QW1S = "ssss"
-QW1W = "a"
-QG = "g"
-QW2W = "s"
-QW2S = "ssss"
-NB = 2
-AV = 2
-AE = 1
-SW1 = 0
-SW2 = 0
-LASTV = 1
-OUT_CHUNKS = ((0,256),(256,512))
+S = 512
+HALF = S // 2
+LINE = 4
+
+COPIES_BY_VECTOR = 2
+B_TILES_FUSED = 1
+Z_COLUMNS_ON_SCALAR = 448
 
 
 def tile_picked_fkcdtrieblerphopd_none_po_kernel(
@@ -71,11 +35,11 @@ def tile_picked_fkcdtrieblerphopd_none_po_kernel(
         keep = ctx.enter_context(tc.tile_pool(name="keep", bufs=1))
         psum = ctx.enter_context(tc.psum_pool(name="psum", bufs=1))
 
-        def tile(shape, dtype, name):
-            return keep.tile(shape, dtype, name=name, align_bytes=64)
+        def tile(shape, dtype, name, tag=None):
+            return keep.tile(shape, dtype, name=name, tag=tag or name, align_bytes=64)
 
-        def tiles(shape, dtype, name):
-            return [tile(shape, dtype, "%s%d" % (name, t)) for t in range(PACK)]
+        def row_tiles(width, name):
+            return [tile([P, width], F32, "%s%d" % (name, t)) for t in range(PACK)]
 
         def load_list(src, name):
             dst = keep.tile([P, S // 16], U16, name=name)
@@ -87,243 +51,215 @@ def tile_picked_fkcdtrieblerphopd_none_po_kernel(
             queue.dma_start(dst[:].bitcast(I32), src[0].rearrange("p n r -> p (n r)").bitcast(I32))
             return dst
 
-        def load_scales(src, name, clears, queues):
+        def load_scales(src, name, clearers):
             dst = tile([P, src.shape[2]], U8, name)
-            share = src.shape[2] // len(clears)
-            for i, clear in enumerate(clears):
-                clear.memset(dst[:, i * share : (i + 1) * share].bitcast(I32), 0)
+            share = src.shape[2] // len(clearers)
+            for i, engine in enumerate(clearers):
+                engine.memset(dst[:, i * share : (i + 1) * share].bitcast(I32), 0)
             for q in range(QUADS):
-                queues[q].dma_start(dst[32 * q : 32 * q + 4, :].bitcast(I32), src[0, 4 * q : 4 * q + 4, :].bitcast(I32))
+                nc.sync.dma_start(
+                    dst[32 * q : 32 * q + 4, :].bitcast(I32), src[0, 4 * q : 4 * q + 4, :].bitcast(I32))
             return dst
 
-        def load_gain(src, name, queue):
+        def load_gain(src, name):
             dst = tile([P, PACK], F32, name)
-            queue.dma_start(dst[:], src.rearrange("(p t) one -> p (t one)", t=PACK))
+            nc.gpsimd.dma_start(dst[:], src.rearrange("(p t) one -> p (t one)", t=PACK))
             return dst
 
-        def deal(src, name, copy):
-            dst = tile([P, S], src.dtype, name)
-            copy(
-                out=dst[:].rearrange("p (t m) -> p t m", t=PACK),
-                in_=src[:].rearrange("p (m t) -> p t m", t=PACK),
-            )
+        def by_row_tile(raw):
+            return raw[:].rearrange("p (m t) -> p t m", t=PACK)
+
+        def deal(raw, name, copy):
+            dst = tile([P, S], raw.dtype, name)
+            copy(out=dst[:].rearrange("p (t m) -> p t m", t=PACK), in_=by_row_tile(raw))
             return dst
 
-        def product(bank, words, scales, t, rhs_words, rhs_scales):
+        def gather_dealt(dst, window, offsets):
+            nc.vector.tensor_copy(
+                out=dst[:].rearrange("p (t m) -> p m t", t=PACK), in_=window[:].indirect(offsets[:]))
+
+        def product(name, bank, words, scales, t, rhs_words, rhs_scales):
+            acc = psum.tile([P, S], F32, name="%s%d" % (name, t), tag=bank)
             cols = slice(P * t, P * (t + 1))
             nc.tensor.matmul_mx(
-                out=bank[:], lhsT=words[:, cols].bitcast(FP8X4), lhsT_scale=scales[:, cols],
+                out=acc[:], lhsT=words[:, cols].bitcast(FP8X4), lhsT_scale=scales[:, cols],
                 rhs=rhs_words[:].bitcast(FP8X4), rhs_scale=rhs_scales[:], start=True, stop=True,
             )
+            return acc
 
-        def interleave(copy, dst, src):
-            copy(
-                out=dst.rearrange("p (c i) t -> p c t i", i=4),
-                in_=src.rearrange("p t (c i) -> p c t i", i=4),
-            )
+        def plain_copy(dst, window, t):
+            if t < COPIES_BY_VECTOR:
+                nc.vector.tensor_copy(out=dst, in_=window[:, :S])
+            else:
+                nc.sync.dma_start(dst, window[:, :S])
 
-        def split_interleave(dst, src, cut):
-            if cut > 0:
-                interleave(nc.scalar.copy, dst[:, :cut, :], src[:, :, :cut])
-            if cut < S:
-                interleave(nc.vector.tensor_copy, dst[:, cut:, :], src[:, :, cut:])
+        def interleave(grouped, rows, on_scalar):
+            width = rows.shape[2]
+            for copy, lo, hi in ((nc.scalar.copy, 0, on_scalar), (nc.vector.tensor_copy, on_scalar, width)):
+                if lo < hi:
+                    copy(
+                        out=grouped[:, lo:hi, :].rearrange("p (c i) t -> p c t i", i=LINE),
+                        in_=rows[:, :, lo:hi].rearrange("p t (c i) -> p c t i", i=LINE),
+                    )
 
         def quantise(words, scales, grouped):
-            nc.vector.quantize_mx(out=words.bitcast(FP8X4), scales=scales, in_=grouped.rearrange("p j t -> p (j t)"))
+            nc.vector.quantize_mx(
+                out=words.bitcast(FP8X4), scales=scales, in_=grouped[:].rearrange("p j t -> p (j t)"))
 
-        Q = {"s": nc.sync, "a": nc.scalar, "g": nc.gpsimd}
+        def quantised(rows, name, on_scalar):
+            grouped = tile([P, S, PACK], BF16, name + "_bf")
+            words = tile([P, S], U32, name + "_words")
+            scales = tile([P, S], U8, name + "_scales")
+            interleave(grouped, rows, on_scalar)
+            quantise(words[:], scales[:], grouped)
+            return words, scales
+
         l_offs = load_list(offs, "l_offs")
-        w1w_raw = load_words(w1_words, "w1w_raw", nc.scalar)
-        xs = load_scales(x_scales, "xs", [nc.vector, nc.gpsimd], [nc.sync] * QUADS)
+        w1_raw = load_words(w1_words, "w1_raw", nc.scalar)
+        xs = load_scales(x_scales, "xs", [nc.vector, nc.gpsimd])
+        l_cand = load_list(cand, "l_cand")
         xw = load_words(x_words, "xw", nc.sync)
-        if CE:
-            l_cand = load_list(cand, "l_cand")
-        gn_t = load_gain(gn, "gn_t", Q[QG])
-        gs_t = load_gain(gs, "gs_t", Q[QG])
-        w1s_raw = load_scales(w1_scales, "w1s_raw", [nc.gpsimd], [Q[c] for c in QW1S])
+        w1s_raw = load_scales(w1_scales, "w1s_raw", [nc.gpsimd])
+        gn_t = load_gain(gn, "gn_t")
+        gs_t = load_gain(gs, "gs_t")
         l2 = load_list(n2, "l2")
         l1 = load_list(n1, "l1")
         l3 = load_list(n3, "l3")
-        if not CE:
-            l_cand = load_list(cand, "l_cand")
         l4 = load_list(n4, "l4")
         l5 = load_list(n5, "l5")
 
-        y_win = tiles([P, 2 * S], F32, "y_win")
+        y_win = row_tiles(2 * S, "y_win")
         for t in range(PACK):
-            (nc.vector if t == 0 else nc.gpsimd).memset(y_win[t][:, S:], 0.0)
+            nc.vector.memset(y_win[t][:, S:], 0.0)
 
-        xq_s = tile([P, S], U8, "xq_s")
-        nc.vector.tensor_copy(out=xq_s[:], in_=xs[:].indirect(l_offs[:]))
-        w1w = deal(w1w_raw, "w1w", nc.scalar.copy if SW1 else nc.vector.tensor_copy)
-        w1s = deal(w1s_raw, "w1s", nc.vector.tensor_copy)
-        xq_w = tile([P, S], U32, "xq_w")
-        nc.vector.tensor_copy(out=xq_w[:], in_=xw[:].indirect(l_offs[:]))
+        xq_scales = tile([P, S], U8, "xq_scales")
+        nc.vector.tensor_copy(out=xq_scales[:], in_=xs[:].indirect(l_offs[:]))
+        w1 = deal(w1_raw, "w1", nc.vector.tensor_copy)
+        xq_words = tile([P, S], U32, "xq_words")
+        nc.vector.tensor_copy(out=xq_words[:], in_=xw[:].indirect(l_offs[:]))
+        w1s_first = tile([P, P], U8, "w1s_first")
+        w1s_rest = tile([P, S], U8, "w1s_rest")
+        nc.vector.tensor_copy(out=w1s_first[:], in_=by_row_tile(w1s_raw)[:, 0, :])
+        nc.vector.tensor_copy(
+            out=w1s_rest[:, P:].rearrange("p (t m) -> p t m", m=P), in_=by_row_tile(w1s_raw)[:, 1:, :])
 
-        st_win = tiles([P, 2 * S], F32, "st_win")
-        a_win = tiles([P, 2 * S], F32, "a_win")
-        b_win = tiles([P, 2 * S], F32, "b_win")
-        s2 = tiles([P, S], F32, "s2")
-        s5 = tiles([P, S], F32, "s5")
-        e = tiles([P, S], F32, "e")
+        st_win = row_tiles(2 * S, "st_win")
+        a_win = row_tiles(2 * S, "a_win")
+        b_win = row_tiles(2 * S, "b_win")
+        y_plain = [st_win[t][:, S:] for t in range(PACK)]
         pa = [a_win[t][:, S:] for t in range(PACK)]
-        if not DINB:
-            dd = [x[:] for x in tiles([P, S], F32, "d")]
-        else:
-            dd = [b_win[t][:, S:] for t in range(PACK)]
+        diff = [b_win[t][:, S:] for t in range(PACK)]
+        mix = row_tiles(S, "mix")
+        pull = row_tiles(S, "pull")
         z = tile([P, PACK, S], F32, "z")
-        z2 = tile([P, PACK, S], F32, "z2")
-        xc_s = tile([P, S], U8, "xc_s")
-        xc_w = keep.tile([P, S], U32, name="xc_w", tag="w1s_raw" if XH else "xc_w", align_bytes=64)
 
-        def f_y(t):
-            y_bank = psum.tile([P, S], F32, name="yb%d" % t, tag="yb%d" % YBK[t])
-            product(y_bank, w1w, w1s, t, xq_w, xq_s)
-            if t == 0:
-                nc.vector.tensor_copy(out=y_win[t][:, :S], in_=y_bank[:])
-            else:
-                nc.scalar.copy(out=y_win[t][:, :S], in_=y_bank[:])
-            nc.sync.dma_start(st_win[t][:, S:], y_win[t][:, :S])
+        def fetch_y(t):
+            acc = product("y", "y", w1, w1s_rest if t else w1s_first, t, xq_words, xq_scales)
+            (nc.scalar.copy if t else nc.vector.tensor_copy)(out=y_win[t][:, :S], in_=acc[:])
+            plain_copy(y_plain[t], y_win[t], t)
 
-        def f_pa(t):
-            if t < PAV:
-                nc.vector.tensor_copy(out=pa[t], in_=y_win[t][:].indirect(l1[:]))
-            else:
-                nc.scalar.activation(out=pa[t], in_=y_win[t][:].indirect(l1[:]), func=ACT.Copy)
+        def pick_mix(t):
+            nc.scalar.activation(out=mix[t][:], in_=y_win[t][:].indirect(l2[:]), func=ACT.Sigmoid)
 
-        def f_s2(t):
-            nc.scalar.activation(out=s2[t][:], in_=y_win[t][:].indirect(l2[:]), func=ACT.Sigmoid)
+        def pick_pa(t):
+            nc.scalar.activation(out=pa[t], in_=y_win[t][:].indirect(l1[:]), func=ACT.Copy)
 
-        def f_d(t):
-            nc.vector.tensor_tensor(out=dd[t], in0=y_win[t][:].indirect(l3[:]), in1=pa[t], op=ALU.subtract)
+        def pick_differences(t):
+            nc.vector.tensor_tensor(out=diff[t], in0=y_win[t][:].indirect(l3[:]), in1=pa[t], op=ALU.subtract)
+            nc.vector.tensor_tensor(
+                out=st_win[t][:, :S], in0=y_win[t][:].indirect(l4[:]), in1=y_plain[t], op=ALU.subtract)
 
-        def f_e(t):
-            nc.vector.scalar_tensor_tensor(out=e[t][:], in0=dd[t], scalar=gn_t[:, t : t + 1], in1=s2[t][:], op0=ALU.mult, op1=ALU.mult)
-
-        def f_z(t):
-            nc.vector.scalar_tensor_tensor(out=z[:, t, :], in0=pa[t], scalar=gn_t[:, t : t + 1], in1=e[t][:], op0=ALU.mult, op1=ALU.add)
-
-        def f_st(t):
-            nc.vector.tensor_tensor(out=st_win[t][:, :S], in0=y_win[t][:].indirect(l4[:]), in1=st_win[t][:, S:], op=ALU.subtract)
-
-        def f_s5(t):
-            nc.scalar.activation(out=s5[t][:], in_=st_win[t][:].indirect(l5[:]), func=ACT.Sigmoid)
-
-        def f_z2(t):
+        def make_pull(t):
             nc.vector.scalar_tensor_tensor(
-                out=z2[:, t, :], in0=y_win[t][:, :S], scalar=gs_t[:, t : t + 1], in1=s5[t][:], op0=ALU.mult, op1=ALU.mult)
+                out=pull[t][:], in0=diff[t], scalar=gn_t[:, t : t + 1], in1=mix[t][:], op0=ALU.mult, op1=ALU.mult)
 
-        f_y(0)
-        f_s2(0)
-        stages = [(f_y, LY), (f_pa, LPA), (f_s2, LS2), (f_d, LD), (f_st, LST), (f_s5, LS5), (f_e, LE), (f_z, LZ), (f_z2, LZ2)]
-        for step in range(-4, 20):
-            for f, lag in stages:
-                t = step - lag
-                if 0 <= t < PACK and not (t == 0 and f in (f_y, f_s2)):
-                    f(t)
-            if step == CANDT:
-                nc.vector.tensor_copy(out=xc_s[:].rearrange("p (t m) -> p m t", t=PACK), in_=xs[:].indirect(l_cand[:]))
-                nc.vector.tensor_copy(out=xc_w[:].rearrange("p (t m) -> p m t", t=PACK), in_=xw[:].indirect(l_cand[:]))
-            if step == W2T:
-                w2w_raw = load_words(w2_words, "w2w_raw", Q[QW2W])
-                w2s_raw = load_scales(w2_scales, "w2s_raw", [nc.gpsimd], [Q[c] for c in QW2S])
-                w2w = deal(w2w_raw, "w2w", nc.scalar.copy if SW2 else nc.vector.tensor_copy)
-                w2s = deal(w2s_raw, "w2s", nc.vector.tensor_copy)
-            if step == ZQ:
-                z_bf = tile([P, S, PACK], BF16, "z_bf")
-                zq_w = tile([P, S], U32, "zq_w")
-                zq_s = tile([P, S], U8, "zq_s")
-                split_interleave(z_bf, z, SPLIT1)
-                quantise(zq_w[:], zq_s[:], z_bf[:])
+        def make_z(t):
+            nc.vector.scalar_tensor_tensor(
+                out=z[:, t, :], in0=pa[t], scalar=gn_t[:, t : t + 1], in1=pull[t][:], op0=ALU.mult, op1=ALU.add)
+
+        fetch_y(0)
+        pick_mix(0)
+        pick_pa(0)
+
+        xc_scales = tile([P, S], U8, "xc_scales")
+        gather_dealt(xc_scales, xs, l_cand)
+        xc_words = tile([P, S], U32, "xc_words", tag="w1s_first")
+        gather_dealt(xc_words, xw, l_cand)
+
+        for step in range(1, PACK + 3):
+            if step < PACK:
+                fetch_y(step)
+                pick_pa(step)
+            if 0 < step - 1 < PACK:
+                pick_mix(step - 1)
+            if step - 1 < PACK:
+                pick_differences(step - 1)
+            if 0 <= step - 2 < PACK:
+                make_pull(step - 2)
+            if 0 <= step - 3:
+                make_z(step - 3)
+
+        w2_raw = load_words(w2_words, "w2_raw", nc.sync)
+        w2s_raw = load_scales(w2_scales, "w2s_raw", [nc.gpsimd])
+        w2 = deal(w2_raw, "w2", nc.scalar.copy)
+        w2s = deal(w2s_raw, "w2s", nc.vector.tensor_copy)
+        z_words, z_scales = quantised(z, "zq", Z_COLUMNS_ON_SCALAR)
+
+        gate2 = row_tiles(S, "gate2")
+        z2 = tile([P, PACK, S], F32, "z2")
+        for t in range(PACK):
+            nc.scalar.activation(out=gate2[t][:], in_=st_win[t][:].indirect(l5[:]), func=ACT.Sigmoid)
+            nc.vector.scalar_tensor_tensor(
+                out=z2[:, t, :], in0=y_win[t][:, :S], scalar=gs_t[:, t : t + 1], in1=gate2[t][:],
+                op0=ALU.mult, op1=ALU.mult)
 
         l6 = load_list(n6, "l6")
         l7 = load_list(n7, "l7")
+        a_plain = row_tiles(S, "a_plain")
+        for t in range(PACK):
+            acc = product("a", "a%d" % t, w2, w2s, t, z_words, z_scales)
+            nc.scalar.copy(out=a_win[t][:, :S], in_=acc[:])
+            plain_copy(a_plain[t][:], a_win[t], t)
 
-        def fetch(t, bank, win, plain, how):
-            (nc.vector.tensor_copy if how in "W" else nc.scalar.copy)(out=win[:, :S], in_=bank[:])
-            if how == "v":
-                nc.vector.tensor_copy(out=plain, in_=win[:, :S])
-            if how in "dW":
-                nc.sync.dma_start(plain, win[:, :S])
-
-        a_plain = tiles([P, S], F32, "a_plain")
-        b_plain = tiles([P, S], F32, "b_plain")
-
-        def f_a(t):
-            a_bank = psum.tile([P, S], F32, name="ab%d" % t, tag="ab%d" % t)
-            product(a_bank, w2w, w2s, t, zq_w, zq_s)
-            fetch(t, a_bank, a_win[t], a_plain[t][:], HA[t])
-
-        for t in range(AE):
-            f_a(t)
-        z2_bf = tile([P, S, PACK], BF16, "z2_bf")
-        z2q_w = tile([P, S], U32, "z2q_w")
-        z2q_s = tile([P, S], U8, "z2q_s")
-        split_interleave(z2_bf, z2, SPLIT2)
-        quantise(z2q_w[:], z2q_s[:], z2_bf[:])
-
-        def f_b(t):
-            b_bank = psum.tile([P, S], F32, name="bb%d" % t, tag="bb%d" % (t % 2))
-            product(b_bank, xc_w, xc_s, t, z2q_w, z2q_s)
-            fetch(t, b_bank, b_win[t], b_plain[t][:], HB[t])
-
-        if BFIRST:
-            for t in range(PACK):
-                f_b(t)
-        for t in range(AE, PACK):
-            f_a(t)
-        if not BFIRST:
-            for t in range(PACK):
-                f_b(t)
-
-        def add_picked(out, spare, win, plain, lst, c0, c1, how):
-            picked = win[:].indirect(lst[:, c0 // 16 : c1 // 16])
-            if how == "s":
-                nc.scalar.activation(out=spare, in_=picked, func=ACT.Copy)
-                nc.vector.tensor_tensor(out=out, in0=spare, in1=win[:, c0:c1], op=ALU.add)
-            else:
-                nc.vector.tensor_tensor(out=out, in0=picked, in1=plain[:, c0:c1], op=ALU.add)
-
-        if not ACH:
-            sa = tile([P, PACK, S], F32, "sa")
-            ga = tile([P, PACK, S], F32, "ga")
-            for t in range(PACK):
-                add_picked(sa[:, t, :], ga[:, t, :], a_win[t], a_plain[t], l6, 0, S, HA[t])
-        if not BCH:
-            sb = tile([P, PACK, S], F32, "sb")
-            gb = tile([P, PACK, S], F32, "gb")
-            for t in range(PACK):
-                add_picked(sb[:, t, :], gb[:, t, :], b_win[t], b_plain[t], l7, 0, S, HB[t])
+        z2_words, z2_scales = quantised(z2, "z2q", HALF)
+        b_plain = [tile([P, S], F32, "b_plain%d" % t) for t in range(B_TILES_FUSED)]
+        for t in range(PACK):
+            acc = product("b", "b%d" % (t % 2), xc_words, xc_scales, t, z2_words, z2_scales)
+            nc.scalar.copy(out=b_win[t][:, :S], in_=acc[:])
+            if t < B_TILES_FUSED:
+                plain_copy(b_plain[t][:], b_win[t], t)
 
         out_rows = out_0.rearrange("(p t) j -> p t j", t=PACK)
         out_words = out_1[0].rearrange("p n r -> p (n r)").bitcast(I32)
-        oq_s = tile([P, S], U8, "oq_s")
-        for c0, c1 in OUT_CHUNKS:
-            w = c1 - c0
-            if not BCH:
-                sbc = sb[:, :, c0:c1]
-            if not ACH:
-                sac = sa[:, :, c0:c1]
-            if BCH:
-                sbc = tile([P, PACK, w], F32, "sb%d" % c0)[:]
-                gbc = keep.tile([P, PACK, w], F32, name="gb%d" % c0, tag=("sb0" if GH == 1 and c0 else "gb%d" % c0), align_bytes=64)
-                for t in range(PACK):
-                    add_picked(sbc[:, t, :], gbc[:, t, :], b_win[t], b_plain[t], l7, c0, c1, HB[t])
-            gate = tile([P, PACK, w], F32, "gate%d" % c0)
-            nc.scalar.activation(out=gate[:], in_=sbc, func=ACT.Sigmoid, scale=0.0625)
-            if ACH:
-                sac = keep.tile([P, PACK, w], F32, name="sa%d" % c0, tag=("sa0" if AH == 1 and c0 else "sb0" if AH == 2 and c0 else "sa%d" % c0), align_bytes=64)[:]
-                gac = tile([P, PACK, w], F32, "ga%d" % c0)
-                for t in range(PACK):
-                    add_picked(sac[:, t, :], gac[:, t, :], a_win[t], a_plain[t], l6, c0, c1, HA[t])
-            res = tile([P, PACK, w], F32, "res%d" % c0)
-            nc.vector.tensor_tensor(out=res[:], in0=sac, in1=gate[:], op=ALU.mult)
-            nc.sync.dma_start(out_rows[:, :, c0:c1], res[:])
-            res_bf = tile([P, w, PACK], BF16, "res_bf%d" % c0)
-            interleave(nc.vector.tensor_copy if c1 == S and LASTV else nc.scalar.copy, res_bf[:], res[:])
-            oq_w = tile([P, w], U32, "oq_w%d" % c0)
-            quantise(oq_w[:], oq_s[:, c0:c1], res_bf[:])
-            nc.sync.dma_start(out_words[:, c0:c1], oq_w[:].bitcast(I32))
+        out_scales = tile([P, S], U8, "out_scales")
+        for lo in range(0, S, HALF):
+            hi = lo + HALF
+            entries = slice(lo // 16, hi // 16)
+            b_sum = tile([P, PACK, HALF], F32, "b_sum%d" % lo)
+            b_picked = tile([P, PACK, HALF], F32, "b_picked%d" % lo)
+            for t in range(PACK):
+                picked = b_win[t][:].indirect(l7[:, entries])
+                if t < B_TILES_FUSED:
+                    nc.vector.tensor_tensor(out=b_sum[:, t, :], in0=picked, in1=b_plain[t][:, lo:hi], op=ALU.add)
+                else:
+                    nc.scalar.activation(out=b_picked[:, t, :], in_=picked, func=ACT.Copy)
+                    nc.vector.tensor_tensor(
+                        out=b_sum[:, t, :], in0=b_picked[:, t, :], in1=b_win[t][:, lo:hi], op=ALU.add)
+            gate = tile([P, PACK, HALF], F32, "gate%d" % lo)
+            nc.scalar.activation(out=gate[:], in_=b_sum[:], func=ACT.Sigmoid, scale=0.0625)
+            a_sum = tile([P, PACK, HALF], F32, "a_sum%d" % lo)
+            for t in range(PACK):
+                nc.vector.tensor_tensor(
+                    out=a_sum[:, t, :], in0=a_win[t][:].indirect(l6[:, entries]), in1=a_plain[t][:, lo:hi],
+                    op=ALU.add)
+            result = tile([P, PACK, HALF], F32, "result%d" % lo)
+            nc.vector.tensor_tensor(out=result[:], in0=a_sum[:], in1=gate[:], op=ALU.mult)
+            nc.sync.dma_start(out_rows[:, :, lo:hi], result[:])
+            result_bf = tile([P, HALF, PACK], BF16, "result_bf%d" % lo)
+            interleave(result_bf, result, HALF // 2 if hi == S else HALF)
+            result_words = tile([P, HALF], U32, "result_words%d" % lo)
+            quantise(result_words[:], out_scales[:, lo:hi], result_bf)
+            nc.sync.dma_start(out_words[:, lo:hi], result_words[:].bitcast(I32))
         for q in range(QUADS):
-            queue = nc.scalar if q % 2 else nc.sync
-            queue.dma_start(out_2[0, 4 * q : 4 * q + 4, :].bitcast(I32), oq_s[32 * q : 32 * q + 4, :].bitcast(I32))
+            (nc.scalar if q % 2 else nc.sync).dma_start(
+                out_2[0, 4 * q : 4 * q + 4, :].bitcast(I32), out_scales[32 * q : 32 * q + 4, :].bitcast(I32))

@@ -69,14 +69,18 @@ def tile_picked_fkcdtrieblerphopd_none_po_kernel(
         def by_row_tile(raw):
             return raw[:].rearrange("p (m t) -> p t m", t=PACK)
 
-        def deal(raw, name, copy):
-            dst = tile([P, S], raw.dtype, name)
-            copy(out=dst[:].rearrange("p (t m) -> p t m", t=PACK), in_=by_row_tile(raw))
+        def deal_scales(raw, name, tag=None):
+            dst = tile([P, S], U8, name, tag)
+            nc.vector.tensor_copy(out=dst[:].rearrange("p (t m) -> p t m", t=PACK), in_=by_row_tile(raw))
             return dst
 
-        def gather_dealt(dst, window, offsets):
-            nc.vector.tensor_copy(
-                out=dst[:].rearrange("p (t m) -> p m t", t=PACK), in_=window[:].indirect(offsets[:]))
+        def deal_words(raw, name, copy):
+            dst = tile([P, S], U32, name)
+            copy(
+                out=dst[:].rearrange("p (t c i) -> p c t i", t=PACK, i=LINE),
+                in_=raw[:].rearrange("p (c i t) -> p c t i", t=PACK, i=LINE),
+            )
+            return dst
 
         def product(name, bank, words, scales, t, rhs_words, rhs_scales):
             acc = psum.tile([P, S], F32, name="%s%d" % (name, t), tag=bank)
@@ -134,7 +138,7 @@ def tile_picked_fkcdtrieblerphopd_none_po_kernel(
 
         xq_scales = tile([P, S], U8, "xq_scales")
         nc.vector.tensor_copy(out=xq_scales[:], in_=xs[:].indirect(l_offs[:]))
-        w1 = deal(w1_raw, "w1", nc.vector.tensor_copy)
+        w1 = deal_words(w1_raw, "w1", nc.vector.tensor_copy)
         xq_words = tile([P, S], U32, "xq_words")
         nc.vector.tensor_copy(out=xq_words[:], in_=xw[:].indirect(l_offs[:]))
         w1s_first = tile([P, P], U8, "w1s_first")
@@ -181,10 +185,13 @@ def tile_picked_fkcdtrieblerphopd_none_po_kernel(
         pick_mix(0)
         pick_pa(0)
 
-        xc_scales = tile([P, S], U8, "xc_scales")
-        gather_dealt(xc_scales, xs, l_cand)
-        xc_words = tile([P, S], U32, "xc_words", tag="w1s_first")
-        gather_dealt(xc_words, xw, l_cand)
+        xc_scales_raw = tile([P, S], U8, "xc_scales_raw")
+        nc.vector.tensor_copy(out=xc_scales_raw[:], in_=xs[:].indirect(l_cand[:]))
+        xc_words_raw = tile([P, S], U32, "xc_words_raw", tag="w1s_first")
+        nc.vector.tensor_copy(out=xc_words_raw[:], in_=xw[:].indirect(l_cand[:]))
+
+        xc_words = deal_words(xc_words_raw, "xc_words", nc.vector.tensor_copy)
+        xc_scales = deal_scales(xc_scales_raw, "xc_scales", "w1s_raw")
 
         for step in range(1, PACK + 3):
             if step < PACK:
@@ -201,8 +208,8 @@ def tile_picked_fkcdtrieblerphopd_none_po_kernel(
 
         w2_raw = load_words(w2_words, "w2_raw", nc.sync)
         w2s_raw = load_scales(w2_scales, "w2s_raw", [nc.gpsimd])
-        w2 = deal(w2_raw, "w2", nc.scalar.copy)
-        w2s = deal(w2s_raw, "w2s", nc.vector.tensor_copy)
+        w2 = deal_words(w2_raw, "w2", nc.scalar.copy)
+        w2s = deal_scales(w2s_raw, "w2s")
         z_words, z_scales = quantised(z, "zq", Z_COLUMNS_ON_SCALAR)
 
         gate2 = row_tiles(S, "gate2")

from contextlib import ExitStack

import concourse.mybir as mybir

FLOPS = 3 * 2 * 512 * 512 * 512

F32 = mybir.dt.float32
BF16 = mybir.dt.bfloat16
I32 = mybir.dt.int32
U32 = mybir.dt.uint32
U16 = mybir.dt.uint16
U8 = mybir.dt.uint8
FP8X4 = mybir.dt.float8_e4m3fn_x4
ACT = mybir.ActivationFunctionType
ALU = mybir.AluOpType

P = 128
PACK = 4
QUADS = 4
S = 512
HALF = S // 2
LINE = 4

COPIES_BY_VECTOR = 2
B_TILES_FUSED = 1
Z_COLUMNS_ON_SCALAR = 448


def tile_picked_fkcdtrieblerphopd_none_po_kernel(
    tc, x_words, x_scales, w1_words, w1_scales, gn, w2_words, w2_scales, gs,
    offs, n1, n2, n3, n4, n5, cand, n6, n7, out_0, out_1, out_2,
):
    nc = tc.nc
    with ExitStack() as ctx:
        keep = ctx.enter_context(tc.tile_pool(name="keep", bufs=1))
        psum = ctx.enter_context(tc.psum_pool(name="psum", bufs=1))

        def tile(shape, dtype, name, tag=None):
            return keep.tile(shape, dtype, name=name, tag=tag or name, align_bytes=64)

        def row_tiles(width, name):
            return [tile([P, width], F32, "%s%d" % (name, t)) for t in range(PACK)]

        def load_list(src, name):
            dst = keep.tile([P, S // 16], U16, name=name)
            nc.sync.dma_start(dst[:], src)
            return dst

        def load_words(src, name, queue):
            dst = tile([P, src.shape[2]], U32, name)
            queue.dma_start(dst[:].bitcast(I32), src[0].rearrange("p n r -> p (n r)").bitcast(I32))
            return dst

        def load_scales(src, name, clearers):
            dst = tile([P, src.shape[2]], U8, name)
            share = src.shape[2] // len(clearers)
            for i, engine in enumerate(clearers):
                engine.memset(dst[:, i * share : (i + 1) * share].bitcast(I32), 0)
            for q in range(QUADS):
                nc.sync.dma_start(
                    dst[32 * q : 32 * q + 4, :].bitcast(I32), src[0, 4 * q : 4 * q + 4, :].bitcast(I32))
            return dst

        def load_gain(src, name):
            dst = tile([P, PACK], F32, name)
            nc.gpsimd.dma_start(dst[:], src.rearrange("(p t) one -> p (t one)", t=PACK))
            return dst

        def by_row_tile(raw):
            return raw[:].rearrange("p (m t) -> p t m", t=PACK)

        def deal_scales(raw, name, tag=None):
            dst = tile([P, S], U8, name, tag)
            nc.vector.tensor_copy(out=dst[:].rearrange("p (t m) -> p t m", t=PACK), in_=by_row_tile(raw))
            return dst

        def deal_words(raw, name, copy):
            dst = tile([P, S], U32, name)
            copy(
                out=dst[:].rearrange("p (t c i) -> p c t i", t=PACK, i=LINE),
                in_=raw[:].rearrange("p (c i t) -> p c t i", t=PACK, i=LINE),
            )
            return dst

        def product(name, bank, words, scales, t, rhs_words, rhs_scales):
            acc = psum.tile([P, S], F32, name="%s%d" % (name, t), tag=bank)
            cols = slice(P * t, P * (t + 1))
            nc.tensor.matmul_mx(
                out=acc[:], lhsT=words[:, cols].bitcast(FP8X4), lhsT_scale=scales[:, cols],
                rhs=rhs_words[:].bitcast(FP8X4), rhs_scale=rhs_scales[:], start=True, stop=True,
            )
            return acc

        def plain_copy(dst, window, t):
            if t < COPIES_BY_VECTOR:
                nc.vector.tensor_copy(out=dst, in_=window[:, :S])
            else:
                nc.sync.dma_start(dst, window[:, :S])

        def interleave(grouped, rows, on_scalar):
            width = rows.shape[2]
            for copy, lo, hi in ((nc.scalar.copy, 0, on_scalar), (nc.vector.tensor_copy, on_scalar, width)):
                if lo < hi:
                    copy(
                        out=grouped[:, lo:hi, :].rearrange("p (c i) t -> p c t i", i=LINE),
                        in_=rows[:, :, lo:hi].rearrange("p t (c i) -> p c t i", i=LINE),
                    )

        def quantise(words, scales, grouped):
            nc.vector.quantize_mx(
                out=words.bitcast(FP8X4), scales=scales, in_=grouped[:].rearrange("p j t -> p (j t)"))

        def quantised(rows, name, on_scalar):
            grouped = tile([P, S, PACK], BF16, name + "_bf")
            words = tile([P, S], U32, name + "_words")
            scales = tile([P, S], U8, name + "_scales")
            interleave(grouped, rows, on_scalar)
            quantise(words[:], scales[:], grouped)
            return words, scales

        l_offs = load_list(offs, "l_offs")
        w1_raw = load_words(w1_words, "w1_raw", nc.scalar)
        xs = load_scales(x_scales, "xs", [nc.vector, nc.gpsimd])
        l_cand = load_list(cand, "l_cand")
        xw = load_words(x_words, "xw", nc.sync)
        w1s_raw = load_scales(w1_scales, "w1s_raw", [nc.gpsimd])
        gn_t = load_gain(gn, "gn_t")
        gs_t = load_gain(gs, "gs_t")
        l2 = load_list(n2, "l2")
        l1 = load_list(n1, "l1")
        l3 = load_list(n3, "l3")
        l4 = load_list(n4, "l4")
        l5 = load_list(n5, "l5")

        y_win = row_tiles(2 * S, "y_win")
        for t in range(PACK):
            nc.vector.memset(y_win[t][:, S:], 0.0)

        xq_scales = tile([P, S], U8, "xq_scales")
        nc.vector.tensor_copy(out=xq_scales[:], in_=xs[:].indirect(l_offs[:]))
        w1 = deal_words(w1_raw, "w1", nc.vector.tensor_copy)
        xq_words = tile([P, S], U32, "xq_words")
        nc.vector.tensor_copy(out=xq_words[:], in_=xw[:].indirect(l_offs[:]))
        w1s_first = tile([P, P], U8, "w1s_first")
        w1s_rest = tile([P, S], U8, "w1s_rest")
        nc.vector.tensor_copy(out=w1s_first[:], in_=by_row_tile(w1s_raw)[:, 0, :])
        nc.vector.tensor_copy(
            out=w1s_rest[:, P:].rearrange("p (t m) -> p t m", m=P), in_=by_row_tile(w1s_raw)[:, 1:, :])

        st_win = row_tiles(2 * S, "st_win")
        a_win = row_tiles(2 * S, "a_win")
        b_win = row_tiles(2 * S, "b_win")
        y_plain = [st_win[t][:, S:] for t in range(PACK)]
        pa = [a_win[t][:, S:] for t in range(PACK)]
        diff = [b_win[t][:, S:] for t in range(PACK)]
        mix = row_tiles(S, "mix")
        pull = row_tiles(S, "pull")
        z = tile([P, PACK, S], F32, "z")

        def fetch_y(t):
            acc = product("y", "y", w1, w1s_rest if t else w1s_first, t, xq_words, xq_scales)
            (nc.scalar.copy if t else nc.vector.tensor_copy)(out=y_win[t][:, :S], in_=acc[:])
            plain_copy(y_plain[t], y_win[t], t)

        def pick_mix(t):
            nc.scalar.activation(out=mix[t][:], in_=y_win[t][:].indirect(l2[:]), func=ACT.Sigmoid)

        def pick_pa(t):
            nc.scalar.activation(out=pa[t], in_=y_win[t][:].indirect(l1[:]), func=ACT.Copy)

        def pick_differences(t):
            nc.vector.tensor_tensor(out=diff[t], in0=y_win[t][:].indirect(l3[:]), in1=pa[t], op=ALU.subtract)
            nc.vector.tensor_tensor(
                out=st_win[t][:, :S], in0=y_win[t][:].indirect(l4[:]), in1=y_plain[t], op=ALU.subtract)

        def make_pull(t):
            nc.vector.scalar_tensor_tensor(
                out=pull[t][:], in0=diff[t], scalar=gn_t[:, t : t + 1], in1=mix[t][:], op0=ALU.mult, op1=ALU.mult)

        def make_z(t):
            nc.vector.scalar_tensor_tensor(
                out=z[:, t, :], in0=pa[t], scalar=gn_t[:, t : t + 1], in1=pull[t][:], op0=ALU.mult, op1=ALU.add)

        fetch_y(0)
        pick_mix(0)
        pick_pa(0)

        xc_scales_raw = tile([P, S], U8, "xc_scales_raw")
        nc.vector.tensor_copy(out=xc_scales_raw[:], in_=xs[:].indirect(l_cand[:]))
        xc_words_raw = tile([P, S], U32, "xc_words_raw", tag="w1s_first")
        nc.vector.tensor_copy(out=xc_words_raw[:], in_=xw[:].indirect(l_cand[:]))

        xc_words = deal_words(xc_words_raw, "xc_words", nc.vector.tensor_copy)
        xc_scales = deal_scales(xc_scales_raw, "xc_scales", "w1s_raw")

        for step in range(1, PACK + 3):
            if step < PACK:
                fetch_y(step)
                pick_pa(step)
            if 0 < step - 1 < PACK:
                pick_mix(step - 1)
            if step - 1 < PACK:
                pick_differences(step - 1)
            if 0 <= step - 2 < PACK:
                make_pull(step - 2)
            if 0 <= step - 3:
                make_z(step - 3)

        w2_raw = load_words(w2_words, "w2_raw", nc.sync)
        w2s_raw = load_scales(w2_scales, "w2s_raw", [nc.gpsimd])
        w2 = deal_words(w2_raw, "w2", nc.scalar.copy)
        w2s = deal_scales(w2s_raw, "w2s")
        z_words, z_scales = quantised(z, "zq", Z_COLUMNS_ON_SCALAR)

        gate2 = row_tiles(S, "gate2")
        z2 = tile([P, PACK, S], F32, "z2")
        for t in range(PACK):
            nc.scalar.activation(out=gate2[t][:], in_=st_win[t][:].indirect(l5[:]), func=ACT.Sigmoid)
            nc.vector.scalar_tensor_tensor(
                out=z2[:, t, :], in0=y_win[t][:, :S], scalar=gs_t[:, t : t + 1], in1=gate2[t][:],
                op0=ALU.mult, op1=ALU.mult)

        l6 = load_list(n6, "l6")
        l7 = load_list(n7, "l7")
        a_plain = row_tiles(S, "a_plain")
        for t in range(PACK):
            acc = product("a", "a%d" % t, w2, w2s, t, z_words, z_scales)
            nc.scalar.copy(out=a_win[t][:, :S], in_=acc[:])
            plain_copy(a_plain[t][:], a_win[t], t)

        z2_words, z2_scales = quantised(z2, "z2q", HALF)
        b_plain = [tile([P, S], F32, "b_plain%d" % t) for t in range(B_TILES_FUSED)]
        for t in range(PACK):
            acc = product("b", "b%d" % (t % 2), xc_words, xc_scales, t, z2_words, z2_scales)
            nc.scalar.copy(out=b_win[t][:, :S], in_=acc[:])
            if t < B_TILES_FUSED:
                plain_copy(b_plain[t][:], b_win[t], t)

        out_rows = out_0.rearrange("(p t) j -> p t j", t=PACK)
        out_words = out_1[0].rearrange("p n r -> p (n r)").bitcast(I32)
        out_scales = tile([P, S], U8, "out_scales")
        for lo in range(0, S, HALF):
            hi = lo + HALF
            entries = slice(lo // 16, hi // 16)
            b_sum = tile([P, PACK, HALF], F32, "b_sum%d" % lo)
            b_picked = tile([P, PACK, HALF], F32, "b_picked%d" % lo)
            for t in range(PACK):
                picked = b_win[t][:].indirect(l7[:, entries])
                if t < B_TILES_FUSED:
                    nc.vector.tensor_tensor(out=b_sum[:, t, :], in0=picked, in1=b_plain[t][:, lo:hi], op=ALU.add)
                else:
                    nc.scalar.activation(out=b_picked[:, t, :], in_=picked, func=ACT.Copy)
                    nc.vector.tensor_tensor(
                        out=b_sum[:, t, :], in0=b_picked[:, t, :], in1=b_win[t][:, lo:hi], op=ALU.add)
            gate = tile([P, PACK, HALF], F32, "gate%d" % lo)
            nc.scalar.activation(out=gate[:], in_=b_sum[:], func=ACT.Sigmoid, scale=0.0625)
            a_sum = tile([P, PACK, HALF], F32, "a_sum%d" % lo)
            for t in range(PACK):
                nc.vector.tensor_tensor(
                    out=a_sum[:, t, :], in0=a_win[t][:].indirect(l6[:, entries]), in1=a_plain[t][:, lo:hi],
                    op=ALU.add)
            result = tile([P, PACK, HALF], F32, "result%d" % lo)
            nc.vector.tensor_tensor(out=result[:], in0=a_sum[:], in1=gate[:], op=ALU.mult)
            nc.sync.dma_start(out_rows[:, :, lo:hi], result[:])
            result_bf = tile([P, HALF, PACK], BF16, "result_bf%d" % lo)
            interleave(result_bf, result, HALF // 2 if hi == S else HALF)
            result_words = tile([P, HALF], U32, "result_words%d" % lo)
            quantise(result_words[:], out_scales[:, lo:hi], result_bf)
            nc.sync.dma_start(out_words[:, lo:hi], result_words[:].bitcast(I32))
        for q in range(QUADS):
            (nc.scalar if q % 2 else nc.sync).dma_start(
                out_2[0, 4 * q : 4 * q + 4, :].bitcast(I32), out_scales[32 * q : 32 * q + 4, :].bitcast(I32))
